import numpy as np
import ml_dtypes


def mxq(x, axis, fmt="e4m3"):
    dtype, down = {"e4m3": (ml_dtypes.float8_e4m3fn, 7), "e5m2": (ml_dtypes.float8_e5m2, 14)}[fmt]
    v = np.moveaxis(np.asarray(x, np.float32).astype(ml_dtypes.bfloat16).astype(np.float64), axis, -1)
    blocks = v.reshape(v.shape[:-1] + (-1, 32))
    amax = np.abs(blocks).max(-1, keepdims=True)
    byte = np.maximum(np.where(amax > 0, np.frexp(amax)[1] - 1 + 127, 0) - down, 1)
    scale = np.exp2(byte - 127.0)
    codes = (blocks / scale).astype(np.float32).astype(dtype).astype(np.float64)
    return np.moveaxis((codes * scale).reshape(v.shape), -1, axis)


WIDE = False


def mx_kscale(k):
    if not WIDE:
        return np.ones(k)
    levels = np.array([10, -10, 5, -5, 0])
    if k % 512:
        return np.exp2(np.random.permutation(np.resize(levels, k // 32))).repeat(32)
    a = np.empty((k // 512, 16))
    for p in range(k // 512):
        a[p, :8] = np.random.permutation(np.resize(levels, 8))
        for g in range(8):
            far = levels[np.abs(levels - a[p, g]) >= 10]
            a[p, g + 8] = far[np.random.randint(len(far))]
    return np.exp2(a.ravel()).repeat(32)


def f64(x):
    return np.asarray(x).astype(np.float64)


def striped(idx):
    return np.tile(idx.reshape(-1, 16).T, (8, 1)).astype(np.uint16)


def unstriped(offs):
    return offs[:16].T.reshape(-1).astype(np.int64)


def pack_weight(w):
    k, n = w.shape
    w = f64(np.asarray(w, np.float32).astype(ml_dtypes.bfloat16)).reshape(k // 32, 32, n)
    amax = np.abs(w).max(1)
    byte = np.clip(np.where(amax > 0, np.frexp(amax)[1] - 1 + 127 - 7, 1), 1, 254)
    scaled = (w * np.exp2(127.0 - byte)[:, None, :]).reshape(k, n).astype(np.float32)
    words = np.ascontiguousarray(scaled.reshape(k // 512, 128, 4, n).transpose(0, 1, 3, 2)).astype(ml_dtypes.float8_e4m3fn).view(np.uint8)
    return words, np.ascontiguousarray(byte.astype(np.uint8).reshape(k // 512, 16, n))


def unpack_weight(words, scales):
    g, p, n, _ = words.shape
    vals = np.ascontiguousarray(words).view(ml_dtypes.float8_e4m3fn).astype(np.float64) * np.repeat(np.exp2(scales.astype(np.float64) - 127.0), 8, axis=1)[..., None]
    return vals.transpose(0, 1, 3, 2).reshape(g * 512, n)


def relu(v):
    return np.maximum(v, 0.0)


K, T, S, V = 512, 2048, 512, 256
P = 2 ** 7


def setup_inputs():
    n = np.random.standard_normal
    s = mx_kscale(K)[:, None]
    packed_xT = pack_weight(n((K, T)) * s)
    return {
        "x_words": packed_xT[0],
        "x_scales": packed_xT[1],
        "hT": (n((K, V)) / np.sqrt(K) / s).astype(np.float32),
        "nn": (np.tile(np.random.uniform(3.0, 4.0, T), (P, 1))).astype(np.float32),
        "own": (np.random.uniform(2.0, 3.0, (V, 1))).astype(np.float32),
        "depot": (np.tile(np.random.uniform(0.5, 3.0, T), (P, 1))).astype(np.float32),
        "dep2": (np.random.uniform(0.5, 3.0, (V, 1))).astype(np.float32),
        "dem": (np.tile(np.random.uniform(0.1, 0.8, T), (P, 1))).astype(np.float32),
        "load": (np.random.uniform(0.1, 0.7, (V, 1))).astype(np.float32),
        "offs": striped(np.random.permutation(T)[:S]),
    }


def reference(x_words, x_scales, hT, nn, own, depot, dep2, dem, load, offs):
    hTq = mxq(f64(hT), 0, "e4m3")
    xq = unpack_weight(x_words, x_scales)[:, unstriped(offs)]
    y = 0.6 * (hTq.T @ xq)
    dist = np.sqrt(f64(nn)[:1][:, unstriped(offs)] - y + f64(own))
    sav = f64(depot)[:1][:, unstriped(offs)] - (1.2 * dist) + f64(dep2)
    ld = f64(dem)[:1][:, unstriped(offs)] + f64(load)
    best = sav.max(axis=1, keepdims=True)
    return sav - (3.0 * ((relu(ld - 0.8)) ** 2)) - (0.5 * best)

@@ -1,0 +1,151 @@
+from contextlib import ExitStack
+
+import concourse.mybir as mybir
+from concourse.masks import make_identity
+
+K, T, S, V = 512, 2048, 512, 256
+FLOPS = 2 * K * S * V
+BYTES = K * T + 16 * T + 4 * K * V + 3 * 4 * T + 3 * 4 * V + 2 * 128 * 32 + 4 * V * S
+
+F32 = mybir.dt.float32
+BF16 = mybir.dt.bfloat16
+I32 = mybir.dt.int32
+U32 = mybir.dt.uint32
+U16 = mybir.dt.uint16
+U8 = mybir.dt.uint8
+FP8X4 = mybir.dt.float8_e4m3fn_x4
+ALU = mybir.AluOpType
+ACT = mybir.ActivationFunctionType
+
+P = 128
+PACK = 4
+HALF = S // 2
+ROW0, ROW_STEP = 8, 4
+
+
+def tile_picked_ysavcw_pen_p_kernel(
+    tc, x_words, x_scales, hT, nn, own, depot, dep2, dem, load, offs, out
+):
+    nc = tc.nc
+    tiles = V // P
+    with ExitStack() as ctx:
+        keep = ctx.enter_context(tc.tile_pool(name="keep", bufs=1))
+        psum = ctx.enter_context(tc.psum_pool(name="psum", bufs=1))
+
+        offsets = keep.tile([P, S // 16], U16, name="offsets")
+        nc.sync.dma_start(offsets[:], offs)
+
+        table_window = keep.tile([P, T], F32, name="table_window", tag="tables_then_x_scale", align_bytes=64)
+        nc.vector.memset(table_window[:].bitcast(I32), 0)
+        scale_window = keep.tile([P, T], U8, name="scale_window", tag="scales_then_h_codes", align_bytes=64)
+        nc.vector.memset(scale_window[:].bitcast(I32), 0)
+
+        def load_scale_rows(queue, q):
+            queue.dma_start(scale_window[32 * q : 32 * q + 4, :].bitcast(I32), x_scales[0, 4 * q : 4 * q + 4, :].bitcast(I32))
+
+        h_raw = keep.tile([P, PACK, V], F32, name="h_raw")
+        nc.scalar.dma_start(h_raw[:], hT.rearrange("(p j) v -> p j v", j=PACK))
+        word_window = keep.tile([P, T], I32, name="word_window", align_bytes=64)
+        nc.scalar.dma_start(word_window[:], x_words[0].rearrange("p c r -> p (c r)").bitcast(I32))
+
+        for r, table in enumerate((nn, depot, dem)):
+            row = ROW0 + ROW_STEP * r
+            nc.sync.dma_start(table_window[row : row + 1, :], table[0:1, :])
+        for q in range(4):
+            load_scale_rows(nc.sync, q)
+
+        identity = keep.tile([P, P], F32, name="identity")
+        make_identity(nc, identity[:])
+        three = keep.tile([P, 1], F32, name="three", tag="three_then_columns")
+        nc.gpsimd.memset(three[:], 3.0)
+        root3 = keep.tile([P, 1], F32, name="root3")
+        nc.scalar.activation(root3[:], three[:], ACT.Sqrt)
+
+        column_tile = keep.tile([P, 3, 8], F32, name="column_tile", tag="three_then_columns")
+        columns = []
+        for r, vec in enumerate((load, own, dep2)):
+            col = column_tile[:, r, 0:tiles]
+            with nc.allow_non_contiguous_dma(reason="one value a partition and row tile"):
+                nc.sync.dma_start(col, vec.rearrange("(a p) o -> p (a o)", p=P))
+            columns.append(col)
+        load_col, own_col, dep2_col = columns
+        load_bias = keep.tile([P, tiles], F32, name="load_bias")
+        nc.gpsimd.tensor_scalar(load_bias[:], load_col, -0.8, 1.0, ALU.add, ALU.mult)
+        own_bias = keep.tile([P, tiles], F32, name="own_bias")
+        nc.gpsimd.tensor_scalar(own_bias[:], own_col, 1.44, 0.0, ALU.mult, ALU.add)
+
+        half_offsets = [offsets[:, h * (HALF // 16) : (h + 1) * (HALF // 16)] for h in range(2)]
+        picked = [keep.tile([P, HALF], F32, name=f"picked{h}") for h in range(2)]
+        turn_bank = [psum.tile([P, 4, P], F32, name=f"turn_bank{h}") for h in range(2)]
+        picked_cols = [keep.tile([P, 2, 3], F32, name=f"picked_cols{h}") for h in range(2)]
+        nn_rows = keep.tile([P, S], F32, name="nn_rows")
+        depot_bank = psum.tile([P, S], F32, name="depot_bank")
+        dem_bank = psum.tile([P, S], F32, name="dem_bank")
+        for h in range(2):
+            nc.vector.tensor_copy(picked[h][:], table_window[:].indirect(half_offsets[h]))
+
+        x_scale = keep.tile([P, S], U8, name="x_scale", tag="tables_then_x_scale", align_bytes=64)
+        nc.vector.tensor_copy(x_scale[:], scale_window[:].indirect(offsets[:]))
+
+        h_grouped = keep.tile([P, V, PACK], BF16, name="h_grouped", tag="h_grouped_then_x_codes", align_bytes=64)
+        nc.scalar.copy(h_grouped[:], h_raw[:].rearrange("p j v -> p v j"))
+
+        for h in range(2):
+            for c in range(2):
+                nc.tensor.transpose(turn_bank[h][:, c, :], picked[h][:, c * P : (c + 1) * P], identity[:])
+            nc.scalar.copy(picked_cols[h][:], turn_bank[h][:, 0:2, ROW0 : ROW0 + 2 * ROW_STEP + 1 : ROW_STEP])
+            for c in range(2):
+                nc.tensor.transpose(turn_bank[h][:, 2 + c, :], picked_cols[h][:, c, 0:1].to_broadcast([P, P]), identity[:])
+            nc.scalar.copy(nn_rows[:, h * HALF : (h + 1) * HALF], turn_bank[h][:, 2:4, :].rearrange("p c n -> p (c n)"))
+        for r, bank in ((2, dem_bank), (1, depot_bank)):
+            for h in range(2):
+                for c in range(2):
+                    j0 = h * HALF + c * P
+                    nc.tensor.transpose(bank[:, j0 : j0 + P], picked_cols[h][:, c, r : r + 1].to_broadcast([P, P]), identity[:])
+
+        h_codes = keep.tile([P, V], U32, name="h_codes", tag="scales_then_h_codes", align_bytes=64)
+        h_scale = keep.tile([P, V], U8, name="h_scale", align_bytes=64)
+        nc.vector.quantize_mx(out=h_codes[:].bitcast(FP8X4), scales=h_scale[:], in_=h_grouped[:].rearrange("p v j -> p (v j)"))
+
+        x_codes = keep.tile([P, S], U32, name="x_codes", tag="h_grouped_then_x_codes", align_bytes=64)
+        for h in range(2):
+            nc.vector.tensor_copy(x_codes[:, h * HALF : (h + 1) * HALF], word_window[:].bitcast(U32).indirect(half_offsets[h]))
+
+        over = [keep.tile([P, S], F32, name=f"over{a}") for a in range(tiles)]
+        for a in range(tiles):
+            nc.scalar.activation(over[a][:], dem_bank[:], ACT.Relu, bias=load_bias[:, a : a + 1])
+
+        spent = [keep.tile([P, S], F32, name=f"spent{a}") for a in range(tiles)]
+        for h in range(2):
+            cols = slice(h * HALF, (h + 1) * HALF)
+            for a in range(tiles):
+                rows = slice(a * P, (a + 1) * P)
+                acc = psum.tile([P, HALF], F32, name=f"acc{h}{a}")
+                nc.tensor.matmul_mx(
+                    out=acc[:],
+                    lhsT=h_codes[:, rows].bitcast(FP8X4),
+                    lhsT_scale=h_scale[:, rows],
+                    rhs=x_codes[:, cols].bitcast(FP8X4),
+                    rhs_scale=x_scale[:, cols],
+                    start=True,
+                    stop=True,
+                )
+                squared = keep.tile([P, HALF], F32, name=f"squared{h}{a}")
+                nc.vector.scalar_tensor_tensor(squared[:], acc[:], -0.6, nn_rows[:, cols], ALU.mult, ALU.add)
+                nc.scalar.activation(spent[a][:, cols], squared[:], ACT.Sqrt, bias=own_bias[:, a : a + 1], scale=1.44)
+
+        penalty = [keep.tile([P, S], F32, name=f"penalty{a}") for a in range(tiles)]
+        for a in range(tiles):
+            nc.scalar.activation(penalty[a][:], over[a][:], ACT.Square, scale=root3[:])
+
+        saving = [keep.tile([P, S], F32, name=f"saving{a}") for a in range(tiles)]
+        halved = [keep.tile([P, S], F32, name=f"halved{a}") for a in range(tiles)]
+        half_best = [keep.tile([P, 1], F32, name=f"half_best{a}") for a in range(tiles)]
+        for a in range(tiles):
+            nc.vector.scalar_tensor_tensor(saving[a][:], depot_bank[:], dep2_col[:, a : a + 1], spent[a][:], ALU.add, ALU.subtract)
+        for a in range(tiles):
+            nc.vector.tensor_scalar(halved[a][:], saving[a][:], 0.5, None, ALU.mult, ALU.max, accum_out=half_best[a][:])
+        for a in range(tiles):
+            result = keep.tile([P, S], F32, name=f"result{a}")
+            nc.vector.scalar_tensor_tensor(result[:], saving[a][:], half_best[a][:], penalty[a][:], ALU.subtract, ALU.subtract)
+            nc.sync.dma_start(out[a * P : (a + 1) * P, :], result[:])

@@ -30,53 +30,51 @@ def tile_picked_ysavcw_pen_p_kernel(
     tiles = V // P
     with ExitStack() as ctx:
         keep = ctx.enter_context(tc.tile_pool(name="keep", bufs=1))
+        early = ctx.enter_context(tc.tile_pool(name="early", bufs=1))
         psum = ctx.enter_context(tc.psum_pool(name="psum", bufs=1))
 
         offsets = keep.tile([P, S // 16], U16, name="offsets")
         nc.sync.dma_start(offsets[:], offs)
 
-        table_window = keep.tile([P, T], F32, name="table_window", tag="tables_then_x_scale", align_bytes=64)
+        def load_column(col, vec):
+            with nc.allow_non_contiguous_dma(reason="one value a partition and row tile"):
+                nc.sync.dma_start(col, vec.rearrange("(a p) o -> p (a o)", p=P))
+
+        load_col = keep.tile([P, tiles], F32, name="load_col")
+        load_column(load_col[:], load)
+        h_raw = keep.tile([P, PACK, V], F32, name="h_raw", tag="h_raw_then_dep2")
+        nc.sync.dma_start(h_raw[:], hT.rearrange("(p j) v -> p j v", j=PACK))
+
+        table_window = early.tile([P, T], F32, name="table_window", offset=0, align_bytes=64)
         nc.vector.memset(table_window[:].bitcast(I32), 0)
-        scale_window = keep.tile([P, T], U8, name="scale_window", tag="scales_then_h_codes", align_bytes=64)
+        scale_window = keep.tile([P, T], U8, name="scale_window", tag="scales_then_x_codes", align_bytes=64)
         nc.vector.memset(scale_window[:].bitcast(I32), 0)
+        three = keep.tile([P, 1], F32, name="three", tag="three_then_words", align_bytes=64)
+        nc.vector.memset(three[:], 3.0)
 
         def load_scale_rows(queue, q):
             queue.dma_start(scale_window[32 * q : 32 * q + 4, :].bitcast(I32), x_scales[0, 4 * q : 4 * q + 4, :].bitcast(I32))
 
-        h_raw = keep.tile([P, PACK, V], F32, name="h_raw")
-        nc.scalar.dma_start(h_raw[:], hT.rearrange("(p j) v -> p j v", j=PACK))
-        word_window = keep.tile([P, T], I32, name="word_window", align_bytes=64)
-        nc.scalar.dma_start(word_window[:], x_words[0].rearrange("p c r -> p (c r)").bitcast(I32))
-
         for r, table in enumerate((nn, depot, dem)):
             row = ROW0 + ROW_STEP * r
             nc.sync.dma_start(table_window[row : row + 1, :], table[0:1, :])
-        for q in range(4):
+        for q in range(3):
             load_scale_rows(nc.sync, q)
+        load_scale_rows(nc.gpsimd, 3)
 
         identity = keep.tile([P, P], F32, name="identity")
         make_identity(nc, identity[:])
-        three = keep.tile([P, 1], F32, name="three", tag="three_then_columns")
-        nc.gpsimd.memset(three[:], 3.0)
         root3 = keep.tile([P, 1], F32, name="root3")
         nc.scalar.activation(root3[:], three[:], ACT.Sqrt)
 
-        column_tile = keep.tile([P, 3, 8], F32, name="column_tile", tag="three_then_columns")
-        columns = []
-        for r, vec in enumerate((load, own, dep2)):
-            col = column_tile[:, r, 0:tiles]
-            with nc.allow_non_contiguous_dma(reason="one value a partition and row tile"):
-                nc.sync.dma_start(col, vec.rearrange("(a p) o -> p (a o)", p=P))
-            columns.append(col)
-        load_col, own_col, dep2_col = columns
+        word_window = keep.tile([P, T], I32, name="word_window", tag="three_then_words", align_bytes=64)
+        nc.sync.dma_start(word_window[:], x_words[0].rearrange("p c r -> p (c r)").bitcast(I32))
         load_bias = keep.tile([P, tiles], F32, name="load_bias")
-        nc.gpsimd.tensor_scalar(load_bias[:], load_col, -0.8, 1.0, ALU.add, ALU.mult)
-        own_bias = keep.tile([P, tiles], F32, name="own_bias")
-        nc.gpsimd.tensor_scalar(own_bias[:], own_col, 1.44, 0.0, ALU.mult, ALU.add)
+        nc.gpsimd.tensor_scalar(load_bias[:], load_col[:], -0.8, 1.0, ALU.add, ALU.mult)
 
         half_offsets = [offsets[:, h * (HALF // 16) : (h + 1) * (HALF // 16)] for h in range(2)]
-        picked = [keep.tile([P, HALF], F32, name=f"picked{h}") for h in range(2)]
-        turn_bank = [psum.tile([P, 4, P], F32, name=f"turn_bank{h}") for h in range(2)]
+        picked = [keep.tile([P, HALF], F32, name=f"picked{h}", tag=f"picked{h}", align_bytes=64) for h in range(2)]
+        turn_bank = [psum.tile([P, S], F32, name=f"turn_bank{h}") for h in range(2)]
         picked_cols = [keep.tile([P, 2, 3], F32, name=f"picked_cols{h}") for h in range(2)]
         nn_rows = keep.tile([P, S], F32, name="nn_rows")
         depot_bank = psum.tile([P, S], F32, name="depot_bank")
@@ -84,38 +82,51 @@ def tile_picked_ysavcw_pen_p_kernel(
         for h in range(2):
             nc.vector.tensor_copy(picked[h][:], table_window[:].indirect(half_offsets[h]))
 
-        x_scale = keep.tile([P, S], U8, name="x_scale", tag="tables_then_x_scale", align_bytes=64)
+        x_scale = early.tile([P, S], U8, name="x_scale", offset=0, align_bytes=64)
         nc.vector.tensor_copy(x_scale[:], scale_window[:].indirect(offsets[:]))
 
-        h_grouped = keep.tile([P, V, PACK], BF16, name="h_grouped", tag="h_grouped_then_x_codes", align_bytes=64)
+        h_grouped = keep.tile([P, V, PACK], BF16, name="h_grouped", align_bytes=64)
         nc.scalar.copy(h_grouped[:], h_raw[:].rearrange("p j v -> p v j"))
+        late_cols = keep.tile([P, 16], F32, name="late_cols", tag="h_raw_then_dep2")
+        own_col, dep2_col = late_cols[:, 0:tiles], late_cols[:, 8 : 8 + tiles]
+        load_column(own_col, own)
+        load_column(dep2_col, dep2)
+        own_bias = keep.tile([P, tiles], F32, name="own_bias")
+        nc.gpsimd.tensor_scalar(own_bias[:], own_col, 1.44, 0.0, ALU.mult, ALU.add)
 
         for h in range(2):
             for c in range(2):
-                nc.tensor.transpose(turn_bank[h][:, c, :], picked[h][:, c * P : (c + 1) * P], identity[:])
-            nc.scalar.copy(picked_cols[h][:], turn_bank[h][:, 0:2, ROW0 : ROW0 + 2 * ROW_STEP + 1 : ROW_STEP])
+                nc.tensor.transpose(turn_bank[h][:, c * P : (c + 1) * P], picked[h][:, c * P : (c + 1) * P], identity[:])
+            nc.scalar.copy(picked_cols[h][:], turn_bank[h][:, 0:HALF].rearrange("p (c n) -> p c n", c=2)[:, :, ROW0 : ROW0 + 2 * ROW_STEP + 1 : ROW_STEP])
             for c in range(2):
-                nc.tensor.transpose(turn_bank[h][:, 2 + c, :], picked_cols[h][:, c, 0:1].to_broadcast([P, P]), identity[:])
-            nc.scalar.copy(nn_rows[:, h * HALF : (h + 1) * HALF], turn_bank[h][:, 2:4, :].rearrange("p c n -> p (c n)"))
+                nc.tensor.transpose(turn_bank[h][:, HALF + c * P : HALF + (c + 1) * P], picked_cols[h][:, c, 0:1].to_broadcast([P, P]), identity[:])
+            nc.scalar.copy(nn_rows[:, h * HALF : (h + 1) * HALF], turn_bank[h][:, HALF:S])
         for r, bank in ((2, dem_bank), (1, depot_bank)):
             for h in range(2):
                 for c in range(2):
                     j0 = h * HALF + c * P
                     nc.tensor.transpose(bank[:, j0 : j0 + P], picked_cols[h][:, c, r : r + 1].to_broadcast([P, P]), identity[:])
 
-        h_codes = keep.tile([P, V], U32, name="h_codes", tag="scales_then_h_codes", align_bytes=64)
+        h_codes = early.tile([P, V], U32, name="h_codes", offset=1024, align_bytes=64)
         h_scale = keep.tile([P, V], U8, name="h_scale", align_bytes=64)
         nc.vector.quantize_mx(out=h_codes[:].bitcast(FP8X4), scales=h_scale[:], in_=h_grouped[:].rearrange("p v j -> p (v j)"))
 
-        x_codes = keep.tile([P, S], U32, name="x_codes", tag="h_grouped_then_x_codes", align_bytes=64)
+        x_codes = keep.tile([P, S], U32, name="x_codes", tag="scales_then_x_codes", align_bytes=64)
         for h in range(2):
             nc.vector.tensor_copy(x_codes[:, h * HALF : (h + 1) * HALF], word_window[:].bitcast(U32).indirect(half_offsets[h]))
 
-        over = [keep.tile([P, S], F32, name=f"over{a}") for a in range(tiles)]
-        for a in range(tiles):
-            nc.scalar.activation(over[a][:], dem_bank[:], ACT.Relu, bias=load_bias[:, a : a + 1])
+        over_tags = ["over0_then_spent", "squared11"]
+        penalty = [keep.tile([P, S], F32, name=f"penalty{a}") for a in range(tiles)]
 
-        spent = [keep.tile([P, S], F32, name=f"spent{a}") for a in range(tiles)]
+        def make_penalty(a):
+            over = keep.tile([P, S], F32, name=f"over{a}", tag=over_tags[a])
+            nc.scalar.activation(over[:], dem_bank[:], ACT.Relu, bias=load_bias[:, a : a + 1])
+            nc.scalar.activation(penalty[a][:], over[:], ACT.Square, scale=root3[:])
+
+        make_penalty(0)
+
+        spent_tile = keep.tile([P, tiles * S], F32, name="spent_tile", tag="over0_then_spent")
+        spent = [spent_tile[:, a * S : (a + 1) * S] for a in range(tiles)]
         for h in range(2):
             cols = slice(h * HALF, (h + 1) * HALF)
             for a in range(tiles):
@@ -130,22 +141,25 @@ def tile_picked_ysavcw_pen_p_kernel(
                     start=True,
                     stop=True,
                 )
-                squared = keep.tile([P, HALF], F32, name=f"squared{h}{a}")
+                squared = keep.tile([P, HALF], F32, name=f"squared{h}{a}", tag=f"squared{h}{a}")
                 nc.vector.scalar_tensor_tensor(squared[:], acc[:], -0.6, nn_rows[:, cols], ALU.mult, ALU.add)
                 nc.scalar.activation(spent[a][:, cols], squared[:], ACT.Sqrt, bias=own_bias[:, a : a + 1], scale=1.44)
 
-        penalty = [keep.tile([P, S], F32, name=f"penalty{a}") for a in range(tiles)]
-        for a in range(tiles):
-            nc.scalar.activation(penalty[a][:], over[a][:], ACT.Square, scale=root3[:])
+        make_penalty(1)
 
         saving = [keep.tile([P, S], F32, name=f"saving{a}") for a in range(tiles)]
         halved = [keep.tile([P, S], F32, name=f"halved{a}") for a in range(tiles)]
         half_best = [keep.tile([P, 1], F32, name=f"half_best{a}") for a in range(tiles)]
+        for h in range(2):
+            cols = slice(h * HALF, (h + 1) * HALF)
+            for a in range(tiles):
+                nc.vector.scalar_tensor_tensor(saving[a][:, cols], depot_bank[:, cols], dep2_col[:, a : a + 1], spent[a][:, cols], ALU.add, ALU.subtract)
+        net = keep.tile([P, S], F32, name="net")
+        nc.gpsimd.tensor_tensor(net[:], saving[0][:], penalty[0][:], ALU.subtract)
         for a in range(tiles):
-            nc.vector.scalar_tensor_tensor(saving[a][:], depot_bank[:], dep2_col[:, a : a + 1], spent[a][:], ALU.add, ALU.subtract)
-        for a in range(tiles):
-            nc.vector.tensor_scalar(halved[a][:], saving[a][:], 0.5, None, ALU.mult, ALU.max, accum_out=half_best[a][:])
-        for a in range(tiles):
-            result = keep.tile([P, S], F32, name=f"result{a}")
-            nc.vector.scalar_tensor_tensor(result[:], saving[a][:], half_best[a][:], penalty[a][:], ALU.subtract, ALU.subtract)
-            nc.sync.dma_start(out[a * P : (a + 1) * P, :], result[:])
+            nc.vector.tensor_scalar(halved[a][:], saving[a][:], -0.5, None, ALU.mult, ALU.min, accum_out=half_best[a][:])
+        result = [keep.tile([P, S], F32, name=f"result{a}") for a in range(tiles)]
+        nc.scalar.activation(result[0][:], net[:], ACT.Identity, bias=half_best[0][:])
+        nc.scalar.dma_start(out[0:P, :], result[0][:])
+        nc.vector.scalar_tensor_tensor(result[1][:], saving[1][:], half_best[1][:], penalty[1][:], ALU.add, ALU.subtract)
+        nc.sync.dma_start(out[P : 2 * P, :], result[1][:])

@@ -1,7 +1,6 @@
 from contextlib import ExitStack
 
 import concourse.mybir as mybir
-from concourse.masks import make_identity
 
 K, T, S, V = 512, 2048, 512, 256
 FLOPS = 2 * K * S * V
@@ -36,76 +35,96 @@ def tile_picked_ysavcw_pen_p_kernel(
         offsets = keep.tile([P, S // 16], U16, name="offsets")
         nc.sync.dma_start(offsets[:], offs)
 
-        def load_column(col, vec):
-            with nc.allow_non_contiguous_dma(reason="one value a partition and row tile"):
-                nc.sync.dma_start(col, vec.rearrange("(a p) o -> p (a o)", p=P))
 
-        load_col = keep.tile([P, tiles], F32, name="load_col")
-        load_column(load_col[:], load)
-        h_raw = keep.tile([P, PACK, V], F32, name="h_raw", tag="h_raw_then_dep2")
+        def load_column(queue, col, vec):
+            with nc.allow_non_contiguous_dma(reason="one value a partition and row tile"):
+                queue.dma_start(col, vec.rearrange("(a p) o -> p (a o)", p=P))
+
+        h_raw = keep.tile([P, PACK, V], F32, name="h_raw", tag="h_raw_then_columns")
         nc.sync.dma_start(h_raw[:], hT.rearrange("(p j) v -> p j v", j=PACK))
 
-        table_window = early.tile([P, T], F32, name="table_window", offset=0, align_bytes=64)
-        nc.vector.memset(table_window[:].bitcast(I32), 0)
         scale_window = keep.tile([P, T], U8, name="scale_window", tag="scales_then_x_codes", align_bytes=64)
         nc.vector.memset(scale_window[:].bitcast(I32), 0)
+        for q, queue in enumerate((nc.gpsimd, nc.sync, nc.sync, nc.sync)):
+            queue.dma_start(scale_window[32 * q : 32 * q + 4, :].bitcast(I32), x_scales[0, 4 * q : 4 * q + 4, :].bitcast(I32))
+        table_window = early.tile([P, T], F32, name="table_window", offset=0, align_bytes=64)
+        nc.vector.memset(table_window[:], 0.0)
         three = keep.tile([P, 1], F32, name="three", tag="three_then_words", align_bytes=64)
         nc.vector.memset(three[:], 3.0)
+        root3 = keep.tile([P, 1], F32, name="root3")
+        nc.scalar.activation(root3[:], three[:], ACT.Sqrt)
+        zeros = keep.tile([P, P], F32, name="zeros", tag="zeros_then_load")
+        nc.vector.memset(zeros[:], 0.0)
+        identity = keep.tile([P, P], F32, name="identity")
+        nc.gpsimd.affine_select(
+            out=identity[:], in_=zeros[:], pattern=[[-1, P]], compare_op=ALU.not_equal, fill=1.0, base=0, channel_multiplier=1
+        )
+        load_col = keep.tile([P, tiles], F32, name="load_col", tag="zeros_then_load")
+        load_column(nc.gpsimd, load_col[:], load)
 
-        def load_scale_rows(queue, q):
-            queue.dma_start(scale_window[32 * q : 32 * q + 4, :].bitcast(I32), x_scales[0, 4 * q : 4 * q + 4, :].bitcast(I32))
 
         for r, table in enumerate((nn, depot, dem)):
             row = ROW0 + ROW_STEP * r
             nc.sync.dma_start(table_window[row : row + 1, :], table[0:1, :])
-        for q in range(3):
-            load_scale_rows(nc.sync, q)
-        load_scale_rows(nc.gpsimd, 3)
-
-        identity = keep.tile([P, P], F32, name="identity")
-        make_identity(nc, identity[:])
-        root3 = keep.tile([P, 1], F32, name="root3")
-        nc.scalar.activation(root3[:], three[:], ACT.Sqrt)
-
         word_window = keep.tile([P, T], I32, name="word_window", tag="three_then_words", align_bytes=64)
         nc.sync.dma_start(word_window[:], x_words[0].rearrange("p c r -> p (c r)").bitcast(I32))
+
         load_bias = keep.tile([P, tiles], F32, name="load_bias")
         nc.gpsimd.tensor_scalar(load_bias[:], load_col[:], -0.8, 1.0, ALU.add, ALU.mult)
 
-        half_offsets = [offsets[:, h * (HALF // 16) : (h + 1) * (HALF // 16)] for h in range(2)]
-        picked = [keep.tile([P, HALF], F32, name=f"picked{h}", tag=f"picked{h}", align_bytes=64) for h in range(2)]
-        turn_bank = [psum.tile([P, S], F32, name=f"turn_bank{h}") for h in range(2)]
-        picked_cols = [keep.tile([P, 2, 3], F32, name=f"picked_cols{h}") for h in range(2)]
-        nn_rows = keep.tile([P, S], F32, name="nn_rows")
-        depot_bank = psum.tile([P, S], F32, name="depot_bank")
-        dem_bank = psum.tile([P, S], F32, name="dem_bank")
-        for h in range(2):
-            nc.vector.tensor_copy(picked[h][:], table_window[:].indirect(half_offsets[h]))
-
-        x_scale = early.tile([P, S], U8, name="x_scale", offset=0, align_bytes=64)
-        nc.vector.tensor_copy(x_scale[:], scale_window[:].indirect(offsets[:]))
-
         h_grouped = keep.tile([P, V, PACK], BF16, name="h_grouped", align_bytes=64)
         nc.scalar.copy(h_grouped[:], h_raw[:].rearrange("p j v -> p v j"))
-        late_cols = keep.tile([P, 16], F32, name="late_cols", tag="h_raw_then_dep2")
+        late_cols = keep.tile([P, 16], F32, name="late_cols", tag="h_raw_then_columns")
         own_col, dep2_col = late_cols[:, 0:tiles], late_cols[:, 8 : 8 + tiles]
-        load_column(own_col, own)
-        load_column(dep2_col, dep2)
+        load_column(nc.sync, own_col, own)
+        load_column(nc.sync, dep2_col, dep2)
         own_bias = keep.tile([P, tiles], F32, name="own_bias")
         nc.gpsimd.tensor_scalar(own_bias[:], own_col, 1.44, 0.0, ALU.mult, ALU.add)
 
+        half_offsets = [offsets[:, h * (HALF // 16) : (h + 1) * (HALF // 16)] for h in range(2)]
+        picked = [keep.tile([P, HALF], F32, name=f"picked{h}") for h in range(2)]
+        for h in range(2):
+            nc.vector.tensor_copy(picked[h][:], table_window[:].indirect(half_offsets[h]))
+        x_scale = early.tile([P, S], U8, name="x_scale", offset=0, align_bytes=64)
+        nc.vector.tensor_copy(x_scale[:], scale_window[:].indirect(offsets[:]))
+
+        turn_bank = [psum.tile([P, S], F32, name=f"turn_bank{h}") for h in range(2)]
+        picked_cols = [keep.tile([P, 2, 3], F32, name=f"picked_cols{h}") for h in range(2)]
         for h in range(2):
             for c in range(2):
                 nc.tensor.transpose(turn_bank[h][:, c * P : (c + 1) * P], picked[h][:, c * P : (c + 1) * P], identity[:])
             nc.scalar.copy(picked_cols[h][:], turn_bank[h][:, 0:HALF].rearrange("p (c n) -> p c n", c=2)[:, :, ROW0 : ROW0 + 2 * ROW_STEP + 1 : ROW_STEP])
+
+        def spread(dst, r, h):
             for c in range(2):
-                nc.tensor.transpose(turn_bank[h][:, HALF + c * P : HALF + (c + 1) * P], picked_cols[h][:, c, 0:1].to_broadcast([P, P]), identity[:])
+                nc.tensor.transpose(dst[:, c * P : (c + 1) * P], picked_cols[h][:, c, r : r + 1].to_broadcast([P, P]), identity[:])
+
+        nn_rows = keep.tile([P, S], F32, name="nn_rows")
+
+        def spread_nn(h):
+            spread(turn_bank[h][:, HALF:S], 0, h)
             nc.scalar.copy(nn_rows[:, h * HALF : (h + 1) * HALF], turn_bank[h][:, HALF:S])
-        for r, bank in ((2, dem_bank), (1, depot_bank)):
-            for h in range(2):
-                for c in range(2):
-                    j0 = h * HALF + c * P
-                    nc.tensor.transpose(bank[:, j0 : j0 + P], picked_cols[h][:, c, r : r + 1].to_broadcast([P, P]), identity[:])
+
+        dem_bank = psum.tile([P, S], F32, name="dem_bank")
+        penalty = [keep.tile([P, S], F32, name=f"penalty{a}") for a in range(tiles)]
+
+        def overload(a, tag):
+            over = keep.tile([P, S], F32, name=f"over{a}", tag=tag)
+            nc.scalar.activation(over[:], dem_bank[:], ACT.Relu, bias=load_bias[:, a : a + 1])
+            return over
+
+        def square(a, over):
+            nc.scalar.activation(penalty[a][:], over[:], ACT.Square, scale=root3[:])
+
+        spread_nn(0)
+        for h in range(2):
+            spread(dem_bank[:, h * HALF : (h + 1) * HALF], 2, h)
+        over0 = overload(0, "over0_then_spent")
+        spread_nn(1)
+        square(0, over0)
+        depot_bank = psum.tile([P, S], F32, name="depot_bank")
+        for h in range(2):
+            spread(depot_bank[:, h * HALF : (h + 1) * HALF], 1, h)
 
         h_codes = early.tile([P, V], U32, name="h_codes", offset=1024, align_bytes=64)
         h_scale = keep.tile([P, V], U8, name="h_scale", align_bytes=64)
@@ -115,23 +134,13 @@ def tile_picked_ysavcw_pen_p_kernel(
         for h in range(2):
             nc.vector.tensor_copy(x_codes[:, h * HALF : (h + 1) * HALF], word_window[:].bitcast(U32).indirect(half_offsets[h]))
 
-        over_tags = ["over0_then_spent", "squared11"]
-        penalty = [keep.tile([P, S], F32, name=f"penalty{a}") for a in range(tiles)]
-
-        def make_penalty(a):
-            over = keep.tile([P, S], F32, name=f"over{a}", tag=over_tags[a])
-            nc.scalar.activation(over[:], dem_bank[:], ACT.Relu, bias=load_bias[:, a : a + 1])
-            nc.scalar.activation(penalty[a][:], over[:], ACT.Square, scale=root3[:])
-
-        make_penalty(0)
-
         spent_tile = keep.tile([P, tiles * S], F32, name="spent_tile", tag="over0_then_spent")
         spent = [spent_tile[:, a * S : (a + 1) * S] for a in range(tiles)]
         for h in range(2):
             cols = slice(h * HALF, (h + 1) * HALF)
             for a in range(tiles):
                 rows = slice(a * P, (a + 1) * P)
-                acc = psum.tile([P, HALF], F32, name=f"acc{h}{a}")
+                acc = psum.tile([P, HALF], F32, name=f"acc{h}{a}", tag=f"acc{h}{a}")
                 nc.tensor.matmul_mx(
                     out=acc[:],
                     lhsT=h_codes[:, rows].bitcast(FP8X4),
@@ -145,7 +154,7 @@ def tile_picked_ysavcw_pen_p_kernel(
                 nc.vector.scalar_tensor_tensor(squared[:], acc[:], -0.6, nn_rows[:, cols], ALU.mult, ALU.add)
                 nc.scalar.activation(spent[a][:, cols], squared[:], ACT.Sqrt, bias=own_bias[:, a : a + 1], scale=1.44)
 
-        make_penalty(1)
+        square(1, overload(1, "squared11"))
 
         saving = [keep.tile([P, S], F32, name=f"saving{a}") for a in range(tiles)]
         halved = [keep.tile([P, S], F32, name=f"halved{a}") for a in range(tiles)]
@@ -154,12 +163,16 @@ def tile_picked_ysavcw_pen_p_kernel(
             cols = slice(h * HALF, (h + 1) * HALF)
             for a in range(tiles):
                 nc.vector.scalar_tensor_tensor(saving[a][:, cols], depot_bank[:, cols], dep2_col[:, a : a + 1], spent[a][:, cols], ALU.add, ALU.subtract)
+        halves = [slice(h * HALF, (h + 1) * HALF) for h in range(2)]
         net = keep.tile([P, S], F32, name="net")
-        nc.gpsimd.tensor_tensor(net[:], saving[0][:], penalty[0][:], ALU.subtract)
+        for cols in halves:
+            nc.gpsimd.tensor_tensor(net[:, cols], saving[0][:, cols], penalty[0][:, cols], ALU.subtract)
         for a in range(tiles):
             nc.vector.tensor_scalar(halved[a][:], saving[a][:], -0.5, None, ALU.mult, ALU.min, accum_out=half_best[a][:])
         result = [keep.tile([P, S], F32, name=f"result{a}") for a in range(tiles)]
-        nc.scalar.activation(result[0][:], net[:], ACT.Identity, bias=half_best[0][:])
-        nc.scalar.dma_start(out[0:P, :], result[0][:])
-        nc.vector.scalar_tensor_tensor(result[1][:], saving[1][:], half_best[1][:], penalty[1][:], ALU.add, ALU.subtract)
-        nc.sync.dma_start(out[P : 2 * P, :], result[1][:])
+        for cols in halves:
+            nc.scalar.activation(result[0][:, cols], net[:, cols], ACT.Identity, bias=half_best[0][:])
+            nc.sync.dma_start(out[0:P, cols], result[0][:, cols])
+        for cols in halves:
+            nc.vector.scalar_tensor_tensor(result[1][:, cols], saving[1][:, cols], half_best[1][:], penalty[1][:, cols], ALU.add, ALU.subtract)
+            nc.sync.dma_start(out[P : 2 * P, cols], result[1][:, cols])

@@ -69,20 +69,15 @@ def tile_picked_ysavcw_pen_p_kernel(
         word_window = keep.tile([P, T], I32, name="word_window", tag="three_then_words", align_bytes=64)
         nc.sync.dma_start(word_window[:], x_words[0].rearrange("p c r -> p (c r)").bitcast(I32))
 
-        load_bias = keep.tile([P, tiles], F32, name="load_bias")
-        nc.gpsimd.tensor_scalar(load_bias[:], load_col[:], -0.8, 1.0, ALU.add, ALU.mult)
-
         h_grouped = keep.tile([P, V, PACK], BF16, name="h_grouped", align_bytes=64)
         nc.scalar.copy(h_grouped[:], h_raw[:].rearrange("p j v -> p v j"))
         late_cols = keep.tile([P, 16], F32, name="late_cols", tag="h_raw_then_columns")
         own_col, dep2_col = late_cols[:, 0:tiles], late_cols[:, 8 : 8 + tiles]
         load_column(nc.sync, own_col, own)
         load_column(nc.sync, dep2_col, dep2)
-        own_bias = keep.tile([P, tiles], F32, name="own_bias")
-        nc.gpsimd.tensor_scalar(own_bias[:], own_col, 1.44, 0.0, ALU.mult, ALU.add)
 
         half_offsets = [offsets[:, h * (HALF // 16) : (h + 1) * (HALF // 16)] for h in range(2)]
-        picked = [keep.tile([P, HALF], F32, name=f"picked{h}") for h in range(2)]
+        picked = [keep.tile([P, HALF], F32, name=f"picked{h}", tag=f"picked{h}") for h in range(2)]
         for h in range(2):
             nc.vector.tensor_copy(picked[h][:], table_window[:].indirect(half_offsets[h]))
         x_scale = early.tile([P, S], U8, name="x_scale", offset=0, align_bytes=64)
@@ -95,6 +90,11 @@ def tile_picked_ysavcw_pen_p_kernel(
                 nc.tensor.transpose(turn_bank[h][:, c * P : (c + 1) * P], picked[h][:, c * P : (c + 1) * P], identity[:])
             nc.scalar.copy(picked_cols[h][:], turn_bank[h][:, 0:HALF].rearrange("p (c n) -> p c n", c=2)[:, :, ROW0 : ROW0 + 2 * ROW_STEP + 1 : ROW_STEP])
 
+        biases = keep.tile([P, 2 * tiles], F32, name="biases", tag="picked1")
+        load_bias, own_bias = biases[:, 0:tiles], biases[:, tiles : 2 * tiles]
+        nc.scalar.activation(load_bias, load_col[:], ACT.Copy, bias=-0.8)
+        nc.scalar.activation(own_bias, own_col, ACT.Copy, scale=1.44)
+
         def spread(dst, r, h):
             for c in range(2):
                 nc.tensor.transpose(dst[:, c * P : (c + 1) * P], picked_cols[h][:, c, r : r + 1].to_broadcast([P, P]), identity[:])
@@ -106,25 +106,19 @@ def tile_picked_ysavcw_pen_p_kernel(
             nc.scalar.copy(nn_rows[:, h * HALF : (h + 1) * HALF], turn_bank[h][:, HALF:S])
 
         dem_bank = psum.tile([P, S], F32, name="dem_bank")
-        penalty = [keep.tile([P, S], F32, name=f"penalty{a}") for a in range(tiles)]
 
-        def overload(a, tag):
-            over = keep.tile([P, S], F32, name=f"over{a}", tag=tag)
-            nc.scalar.activation(over[:], dem_bank[:], ACT.Relu, bias=load_bias[:, a : a + 1])
-            return over
-
-        def square(a, over):
-            nc.scalar.activation(penalty[a][:], over[:], ACT.Square, scale=root3[:])
+        def square(a, over, tag):
+            squared_over = keep.tile([P, S], F32, name=f"penalty{a}", tag=tag)
+            nc.scalar.activation(squared_over[:], over[:], ACT.Square, scale=root3[:])
+            return squared_over
 
         spread_nn(0)
         for h in range(2):
             spread(dem_bank[:, h * HALF : (h + 1) * HALF], 2, h)
-        over0 = overload(0, "over0_then_spent")
+        over0 = keep.tile([P, S], F32, name="over0", tag="over0_then_spent")
+        nc.scalar.activation(over0[:], dem_bank[:], ACT.Relu, bias=load_bias[:, 0:1])
         spread_nn(1)
-        square(0, over0)
-        depot_bank = psum.tile([P, S], F32, name="depot_bank")
-        for h in range(2):
-            spread(depot_bank[:, h * HALF : (h + 1) * HALF], 1, h)
+        penalty = [square(0, over0, "penalty0")]
 
         h_codes = early.tile([P, V], U32, name="h_codes", offset=1024, align_bytes=64)
         h_scale = keep.tile([P, V], U8, name="h_scale", align_bytes=64)
@@ -133,6 +127,9 @@ def tile_picked_ysavcw_pen_p_kernel(
         x_codes = keep.tile([P, S], U32, name="x_codes", tag="scales_then_x_codes", align_bytes=64)
         for h in range(2):
             nc.vector.tensor_copy(x_codes[:, h * HALF : (h + 1) * HALF], word_window[:].bitcast(U32).indirect(half_offsets[h]))
+
+        over1 = keep.tile([P, S], F32, name="over1", tag="over1_then_result")
+        nc.vector.tensor_scalar(over1[:], dem_bank[:], load_bias[:, 1:2], 0.0, ALU.add, ALU.max)
 
         spent_tile = keep.tile([P, tiles * S], F32, name="spent_tile", tag="over0_then_spent")
         spent = [spent_tile[:, a * S : (a + 1) * S] for a in range(tiles)]
@@ -154,7 +151,10 @@ def tile_picked_ysavcw_pen_p_kernel(
                 nc.vector.scalar_tensor_tensor(squared[:], acc[:], -0.6, nn_rows[:, cols], ALU.mult, ALU.add)
                 nc.scalar.activation(spent[a][:, cols], squared[:], ACT.Sqrt, bias=own_bias[:, a : a + 1], scale=1.44)
 
-        square(1, overload(1, "squared11"))
+        depot_rows = [psum.tile([P, HALF], F32, name=f"depot_rows{h}", tag=f"acc0{h}") for h in range(2)]
+        for h in range(2):
+            spread(depot_rows[h][:], 1, h)
+        penalty.append(square(1, over1, "squared11"))
 
         saving = [keep.tile([P, S], F32, name=f"saving{a}") for a in range(tiles)]
         halved = [keep.tile([P, S], F32, name=f"halved{a}") for a in range(tiles)]
@@ -162,14 +162,14 @@ def tile_picked_ysavcw_pen_p_kernel(
         for h in range(2):
             cols = slice(h * HALF, (h + 1) * HALF)
             for a in range(tiles):
-                nc.vector.scalar_tensor_tensor(saving[a][:, cols], depot_bank[:, cols], dep2_col[:, a : a + 1], spent[a][:, cols], ALU.add, ALU.subtract)
+                nc.vector.scalar_tensor_tensor(saving[a][:, cols], depot_rows[h][:], dep2_col[:, a : a + 1], spent[a][:, cols], ALU.add, ALU.subtract)
         halves = [slice(h * HALF, (h + 1) * HALF) for h in range(2)]
         net = keep.tile([P, S], F32, name="net")
         for cols in halves:
             nc.gpsimd.tensor_tensor(net[:, cols], saving[0][:, cols], penalty[0][:, cols], ALU.subtract)
         for a in range(tiles):
             nc.vector.tensor_scalar(halved[a][:], saving[a][:], -0.5, None, ALU.mult, ALU.min, accum_out=half_best[a][:])
-        result = [keep.tile([P, S], F32, name=f"result{a}") for a in range(tiles)]
+        result = [keep.tile([P, S], F32, name="result0", tag="over1_then_result"), keep.tile([P, S], F32, name="result1")]
         for cols in halves:
             nc.scalar.activation(result[0][:, cols], net[:, cols], ACT.Identity, bias=half_best[0][:])
             nc.sync.dma_start(out[0:P, cols], result[0][:, cols])

from contextlib import ExitStack

import concourse.mybir as mybir

K, T, S, V = 512, 2048, 512, 256
FLOPS = 2 * K * S * V
BYTES = K * T + 16 * T + 4 * K * V + 3 * 4 * T + 3 * 4 * V + 2 * 128 * 32 + 4 * V * S

F32 = mybir.dt.float32
BF16 = mybir.dt.bfloat16
I32 = mybir.dt.int32
U32 = mybir.dt.uint32
U16 = mybir.dt.uint16
U8 = mybir.dt.uint8
FP8X4 = mybir.dt.float8_e4m3fn_x4
ALU = mybir.AluOpType
ACT = mybir.ActivationFunctionType

P = 128
PACK = 4
HALF = S // 2
ROW0, ROW_STEP = 8, 4


def tile_picked_ysavcw_pen_p_kernel(
    tc, x_words, x_scales, hT, nn, own, depot, dep2, dem, load, offs, out
):
    nc = tc.nc
    tiles = V // P
    with ExitStack() as ctx:
        keep = ctx.enter_context(tc.tile_pool(name="keep", bufs=1))
        early = ctx.enter_context(tc.tile_pool(name="early", bufs=1))
        psum = ctx.enter_context(tc.psum_pool(name="psum", bufs=1))

        offsets = keep.tile([P, S // 16], U16, name="offsets")
        nc.sync.dma_start(offsets[:], offs)


        def load_column(queue, col, vec):
            with nc.allow_non_contiguous_dma(reason="one value a partition and row tile"):
                queue.dma_start(col, vec.rearrange("(a p) o -> p (a o)", p=P))

        h_raw = keep.tile([P, PACK, V], F32, name="h_raw", tag="h_raw_then_columns")
        nc.sync.dma_start(h_raw[:], hT.rearrange("(p j) v -> p j v", j=PACK))

        scale_window = keep.tile([P, T], U8, name="scale_window", tag="scales_then_x_codes", align_bytes=64)
        nc.vector.memset(scale_window[:].bitcast(I32), 0)
        for q, queue in enumerate((nc.gpsimd, nc.sync, nc.sync, nc.sync)):
            queue.dma_start(scale_window[32 * q : 32 * q + 4, :].bitcast(I32), x_scales[0, 4 * q : 4 * q + 4, :].bitcast(I32))
        table_window = early.tile([P, T], F32, name="table_window", offset=0, align_bytes=64)
        nc.vector.memset(table_window[:], 0.0)
        three = keep.tile([P, 1], F32, name="three", tag="three_then_words", align_bytes=64)
        nc.vector.memset(three[:], 3.0)
        root3 = keep.tile([P, 1], F32, name="root3")
        nc.scalar.activation(root3[:], three[:], ACT.Sqrt)
        zeros = keep.tile([P, P], F32, name="zeros", tag="zeros_then_load")
        nc.vector.memset(zeros[:], 0.0)
        identity = keep.tile([P, P], F32, name="identity")
        nc.gpsimd.affine_select(
            out=identity[:], in_=zeros[:], pattern=[[-1, P]], compare_op=ALU.not_equal, fill=1.0, base=0, channel_multiplier=1
        )
        load_col = keep.tile([P, tiles], F32, name="load_col", tag="zeros_then_load")
        load_column(nc.gpsimd, load_col[:], load)


        for r, table in enumerate((nn, depot, dem)):
            row = ROW0 + ROW_STEP * r
            nc.sync.dma_start(table_window[row : row + 1, :], table[0:1, :])
        word_window = keep.tile([P, T], I32, name="word_window", tag="three_then_words", align_bytes=64)
        nc.sync.dma_start(word_window[:], x_words[0].rearrange("p c r -> p (c r)").bitcast(I32))

        h_grouped = keep.tile([P, V, PACK], BF16, name="h_grouped", align_bytes=64)
        nc.scalar.copy(h_grouped[:], h_raw[:].rearrange("p j v -> p v j"))
        late_cols = keep.tile([P, 16], F32, name="late_cols", tag="h_raw_then_columns")
        own_col, dep2_col = late_cols[:, 0:tiles], late_cols[:, 8 : 8 + tiles]
        load_column(nc.sync, own_col, own)
        load_column(nc.sync, dep2_col, dep2)

        half_offsets = [offsets[:, h * (HALF // 16) : (h + 1) * (HALF // 16)] for h in range(2)]
        picked = [keep.tile([P, HALF], F32, name=f"picked{h}", tag=f"picked{h}") for h in range(2)]
        for h in range(2):
            nc.vector.tensor_copy(picked[h][:], table_window[:].indirect(half_offsets[h]))
        x_scale = early.tile([P, S], U8, name="x_scale", offset=0, align_bytes=64)
        nc.vector.tensor_copy(x_scale[:], scale_window[:].indirect(offsets[:]))

        turn_bank = [psum.tile([P, S], F32, name=f"turn_bank{h}") for h in range(2)]
        picked_cols = [keep.tile([P, 2, 3], F32, name=f"picked_cols{h}") for h in range(2)]
        for h in range(2):
            for c in range(2):
                nc.tensor.transpose(turn_bank[h][:, c * P : (c + 1) * P], picked[h][:, c * P : (c + 1) * P], identity[:])
            nc.scalar.copy(picked_cols[h][:], turn_bank[h][:, 0:HALF].rearrange("p (c n) -> p c n", c=2)[:, :, ROW0 : ROW0 + 2 * ROW_STEP + 1 : ROW_STEP])

        biases = keep.tile([P, 2 * tiles], F32, name="biases", tag="picked1")
        load_bias, own_bias = biases[:, 0:tiles], biases[:, tiles : 2 * tiles]
        nc.scalar.activation(load_bias, load_col[:], ACT.Copy, bias=-0.8)
        nc.scalar.activation(own_bias, own_col, ACT.Copy, scale=1.44)

        def spread(dst, r, h):
            for c in range(2):
                nc.tensor.transpose(dst[:, c * P : (c + 1) * P], picked_cols[h][:, c, r : r + 1].to_broadcast([P, P]), identity[:])

        nn_rows = keep.tile([P, S], F32, name="nn_rows")

        def spread_nn(h):
            spread(turn_bank[h][:, HALF:S], 0, h)
            nc.scalar.copy(nn_rows[:, h * HALF : (h + 1) * HALF], turn_bank[h][:, HALF:S])

        dem_bank = psum.tile([P, S], F32, name="dem_bank")

        def square(a, over, tag):
            squared_over = keep.tile([P, S], F32, name=f"penalty{a}", tag=tag)
            nc.scalar.activation(squared_over[:], over[:], ACT.Square, scale=root3[:])
            return squared_over

        spread_nn(0)
        for h in range(2):
            spread(dem_bank[:, h * HALF : (h + 1) * HALF], 2, h)
        over0 = keep.tile([P, S], F32, name="over0", tag="over0_then_spent")
        nc.scalar.activation(over0[:], dem_bank[:], ACT.Relu, bias=load_bias[:, 0:1])
        spread_nn(1)
        penalty = [square(0, over0, "penalty0")]

        h_codes = early.tile([P, V], U32, name="h_codes", offset=1024, align_bytes=64)
        h_scale = keep.tile([P, V], U8, name="h_scale", align_bytes=64)
        nc.vector.quantize_mx(out=h_codes[:].bitcast(FP8X4), scales=h_scale[:], in_=h_grouped[:].rearrange("p v j -> p (v j)"))

        x_codes = keep.tile([P, S], U32, name="x_codes", tag="scales_then_x_codes", align_bytes=64)
        for h in range(2):
            nc.vector.tensor_copy(x_codes[:, h * HALF : (h + 1) * HALF], word_window[:].bitcast(U32).indirect(half_offsets[h]))

        over1 = keep.tile([P, S], F32, name="over1", tag="over1_then_result")
        nc.vector.tensor_scalar(over1[:], dem_bank[:], load_bias[:, 1:2], 0.0, ALU.add, ALU.max)

        spent_tile = keep.tile([P, tiles * S], F32, name="spent_tile", tag="over0_then_spent")
        spent = [spent_tile[:, a * S : (a + 1) * S] for a in range(tiles)]
        for h in range(2):
            cols = slice(h * HALF, (h + 1) * HALF)
            for a in range(tiles):
                rows = slice(a * P, (a + 1) * P)
                acc = psum.tile([P, HALF], F32, name=f"acc{h}{a}", tag=f"acc{h}{a}")
                nc.tensor.matmul_mx(
                    out=acc[:],
                    lhsT=h_codes[:, rows].bitcast(FP8X4),
                    lhsT_scale=h_scale[:, rows],
                    rhs=x_codes[:, cols].bitcast(FP8X4),
                    rhs_scale=x_scale[:, cols],
                    start=True,
                    stop=True,
                )
                squared = keep.tile([P, HALF], F32, name=f"squared{h}{a}", tag=f"squared{h}{a}")
                nc.vector.scalar_tensor_tensor(squared[:], acc[:], -0.6, nn_rows[:, cols], ALU.mult, ALU.add)
                nc.scalar.activation(spent[a][:, cols], squared[:], ACT.Sqrt, bias=own_bias[:, a : a + 1], scale=1.44)

        depot_rows = [psum.tile([P, HALF], F32, name=f"depot_rows{h}", tag=f"acc0{h}") for h in range(2)]
        for h in range(2):
            spread(depot_rows[h][:], 1, h)
        penalty.append(square(1, over1, "squared11"))

        saving = [keep.tile([P, S], F32, name=f"saving{a}") for a in range(tiles)]
        halved = [keep.tile([P, S], F32, name=f"halved{a}") for a in range(tiles)]
        half_best = [keep.tile([P, 1], F32, name=f"half_best{a}") for a in range(tiles)]
        for h in range(2):
            cols = slice(h * HALF, (h + 1) * HALF)
            for a in range(tiles):
                nc.vector.scalar_tensor_tensor(saving[a][:, cols], depot_rows[h][:], dep2_col[:, a : a + 1], spent[a][:, cols], ALU.add, ALU.subtract)
        halves = [slice(h * HALF, (h + 1) * HALF) for h in range(2)]
        net = keep.tile([P, S], F32, name="net")
        for cols in halves:
            nc.gpsimd.tensor_tensor(net[:, cols], saving[0][:, cols], penalty[0][:, cols], ALU.subtract)
        for a in range(tiles):
            nc.vector.tensor_scalar(halved[a][:], saving[a][:], -0.5, None, ALU.mult, ALU.min, accum_out=half_best[a][:])
        result = [keep.tile([P, S], F32, name="result0", tag="over1_then_result"), keep.tile([P, S], F32, name="result1")]
        for cols in halves:
            nc.scalar.activation(result[0][:, cols], net[:, cols], ACT.Identity, bias=half_best[0][:])
            nc.sync.dma_start(out[0:P, cols], result[0][:, cols])
        for cols in halves:
            nc.vector.scalar_tensor_tensor(result[1][:, cols], saving[1][:, cols], half_best[1][:], penalty[1][:, cols], ALU.add, ALU.subtract)
            nc.sync.dma_start(out[P : 2 * P, cols], result[1][:, cols])
